import numpy as np, ml_dtypes
CORES = [16,32,48,64,80]
N = 5
import mx_ref
NC, G = 256, 4
C = np.float32(0.041)
WID = [160,256,256,128,224]
BF = ml_dtypes.bfloat16
def cut(t, i, w=512):
    return t[:, w * i:w * i + w]
def tile(rs):
    return np.stack(rs, axis=2).reshape(128, -1).astype(BF)
def layer(w, X):
    out = []
    for i in range(G):
        for t in range(len(X)):
            p = mx_ref.matmul(mx_ref.quantize(cut(w, len(X) * i + t)), X[t])
            z = p if t == 0 else z + p
        out.append(z)
    return out
def act(Z):
    return [np.maximum(z, 0) * C for z in Z]
def setup_inputs(rng):
    def f(*shape):
        return mx_ref.flush((rng.standard_normal(shape, dtype=np.float32) * np.exp2(rng.integers(-2, 3, shape[:-1] + (1,)))).astype(BF))
    return {"x": f(N, 128, 4 * NC), "w1": f(N, 128, G * 512), "w2": f(N, 128, 512)}
def setup_inputs_blocks(rng):
    d = setup_inputs(rng)
    for k in ("x", "w1", "w2"): d[k] = mx_ref.spread(d[k], rng, 2)
    return d
def setup_inputs_wide(rng):
    d = setup_inputs(rng)
    for k in ("x", "w1", "w2"): d[k] = mx_ref.flush((d[k].astype(np.float32) * np.exp2(rng.integers(-6, 7, (N, 1, 1))).astype(np.float32)).astype(BF))
    return d
def reference(x, w1, w2):
    X = [mx_ref.quantize(x[j][:, :4 * WID[j]]) for j in range(N)]
    y = np.full((N, 128, NC), np.nan, np.float32)
    for c in range(N):
        for r in range(N):
            p = mx_ref.matmul(mx_ref.quantize(w2[r]), mx_ref.quantize(tile(act(layer(w1[r], [X[c]])))))
            z = p if r == 0 else z + p
        y[c][:, :WID[c]] = z
    return {"y": y}

@@ -1,0 +1,172 @@
+import numpy as np
+from concourse.bass import DstId, RemoteDMATransfer
+from concourse.mybir import dt, AluOpType, ActivationFunctionType
+
+NR = 5
+WMAX = 256
+G = 4
+C = float(np.float32(0.041))
+BANK = 512
+
+SCRATCH = {
+    "xt": ("sbuf", [128, 4 * WMAX], "bfloat16"),
+    "w1t": ("sbuf", [128, G * 512], "bfloat16"),
+    "w2t": ("sbuf", [128, 512], "bfloat16"),
+    "w1q": ("sbuf", [128, G * 128], "float8_e4m3fn_x4"),
+    "w1s": ("sbuf", [128, G * 128], "uint8"),
+    "w2q": ("sbuf", [128, 128], "float8_e4m3fn_x4"),
+    "w2s": ("sbuf", [128, 128], "uint8"),
+    "acc0": ("sbuf", [128, WMAX], "float32"),
+    "acc1": ("sbuf", [128, WMAX], "float32"),
+    "ps": ("psum", [128, 8 * BANK], "float32"),
+}
+for _k in range(NR):
+    SCRATCH["xq%d" % _k] = ("sbuf", [128, WMAX], "float8_e4m3fn_x4")
+    SCRATCH["xs%d" % _k] = ("sbuf", [128, WMAX], "uint8")
+    SCRATCH["h%d" % _k] = ("sbuf", [128, 4 * WMAX], "bfloat16")
+    SCRATCH["hq%d" % _k] = ("sbuf", [128, WMAX], "float8_e4m3fn_x4")
+    SCRATCH["hs%d" % _k] = ("sbuf", [128, WMAX], "uint8")
+    SCRATCH["res%d" % _k] = ("sbuf", [128, WMAX], "float32")
+    SCRATCH["land%d" % _k] = ("sbuf", [128, WMAX], "float32")
+
+SEMAPHORES = ["ldx", "ldw1", "ldw2", "pe", "act", "dve", "sent", "stored"]
+SEMAPHORES += ["x%d" % k for k in range(NR)] + ["y%d" % k for k in range(NR)]
+
+
+def engines(mask):
+    return bin(mask).count("1")
+
+
+def rank_program(g, core, T, topo):
+    r = T.rank_of(core)
+    if r is None:
+        return
+    WID = T.tables["WID"]
+    W = WID[r]
+    to = [(r + k) % NR for k in range(NR)]
+    frm = [(r - k) % NR for k in range(NR)]
+    cnt = {"pe": 0, "act": 0, "dve": 0, "sent": 0}
+    v, s, t = g.vector, g.scalar, g.tensor
+
+    def done(ins, sem):
+        ins.then_inc(T.sem[sem], 1)
+        cnt[sem] += 1
+        return cnt[sem]
+
+    def bank(i, n):
+        return T.ps[:, BANK * i:BANK * i + n]
+
+    g.sync.dma_start(T.xt[:, :4 * W], T.x[:, :4 * W]).then_inc(T.sem.ldx, 16)
+    g.sync.dma_start(T.w1t[:], T.w1[:]).then_inc(T.sem.ldw1, 16)
+    g.sync.dma_start(T.w2t[:], T.w2[:]).then_inc(T.sem.ldw2, 16)
+
+    xq, xs = T["xq%d" % r], T["xs%d" % r]
+    v.wait_ge(T.sem.ldx, 16)
+    x_ready = done(v.quantize_mx(xq[:, :W], xs[:, :W], T.xt[:, :4 * W]), "dve")
+    v.wait_ge(T.sem.ldw1, 16)
+    w1_ready = [done(v.quantize_mx(T.w1q[:, 128 * b:128 * b + 128], T.w1s[:, 128 * b:128 * b + 128],
+                                   T.w1t[:, 512 * b:512 * b + 512]), "dve") for b in range(G)]
+    v.wait_ge(T.sem.ldw2, 16)
+    done(v.quantize_mx(T.w2q[:], T.w2s[:], T.w2t[:]), "dve")
+
+    g.wait_ge(T.sem.dve, x_ready)
+    dst = [T.cores[d] for d in to]
+    rid = [topo.addr(c)[0] for c in dst]
+    pid = [topo.addr(c)[1] for c in dst]
+    msk = [0] + [topo.mask(core, dst[k]) for k in range(1, NR)]
+    every = msk[1]
+    for k in range(2, NR):
+        every &= msk[k]
+    g.remote_dma_fused([RemoteDMATransfer(
+        dst_ids=[DstId(rid=rid[k], pnc=pid[k]) for k in range(1, NR)], dma_engine_mask=every,
+        remote_sem=T.sem["x%d" % r], srcs=[xs[:, :W]], dsts=[xs[:, :W] for k in range(1, NR)])], local_sem=T.sem.sent)
+    cnt["sent"] += engines(every)
+    for k in range(1, NR):
+        g.remote_dma(xq[:, :W].bitcast(dt.uint8), xq[:, :W].bitcast(dt.uint8), T.sem["x%d" % r], T.sem.sent,
+                     pid[k], rid[k], msk[k])
+        cnt["sent"] += engines(msk[k])
+
+    z_done = [[0] * G for k in range(NR)]
+    act_done = [[None] * G for k in range(NR)]
+    q_done = [0] * NR
+    y_done = [0] * NR
+    cp_done = [0] * NR
+
+    def first_product(k):
+        c = frm[k]
+        n = WID[c]
+        if k:
+            sender = T.cores[c]
+            em = topo.mask(sender, core)
+            for o in T.cores:
+                if o != sender:
+                    em &= topo.mask(sender, o)
+            t.wait_ge(T.sem["x%d" % c], engines(em) + engines(topo.mask(sender, core)))
+        for b in range(G):
+            if k == 0:
+                t.wait_ge(T.sem.dve, w1_ready[b])
+            else:
+                sem, val = act_done[k - 1][b]
+                t.wait_ge(T.sem[sem], val)
+            z_done[k][b] = done(t.matmul_mx(bank(b, n), T.w1q[:, 128 * b:128 * b + 128], T.w1s[:, 128 * b:128 * b + 128],
+                                            T["xq%d" % c][:, :n], T["xs%d" % c][:, :n], True, True), "pe")
+
+    def make_h(k):
+        c = frm[k]
+        n = WID[c]
+        h = T["h%d" % c]
+        for b in range(G):
+            if b % 2 == 0:
+                s.wait_ge(T.sem.pe, z_done[k][b])
+                act_done[k][b] = ("act", done(s.activation(h[:, b:4 * n:4], bank(b, n), ActivationFunctionType.Relu,
+                                                           scale=C), "act"))
+            else:
+                v.wait_ge(T.sem.pe, z_done[k][b])
+                act_done[k][b] = ("dve", done(v.tensor_scalar(h[:, b:4 * n:4], bank(b, n), 0.0, C,
+                                                              AluOpType.max, AluOpType.mult), "dve"))
+        v.wait_ge(T.sem.act, cnt["act"])
+        v.wait_ge(T.sem.dve, cnt["dve"])
+        q_done[k] = done(v.quantize_mx(T["hq%d" % c][:, :n], T["hs%d" % c][:, :n], h[:, :4 * n]), "dve")
+
+    def out_bank(k):
+        return G if k == 0 else G + 1 + (k - 1) % (7 - G)
+
+    def second_product(k):
+        c = frm[k]
+        n = WID[c]
+        t.wait_ge(T.sem.dve, q_done[k])
+        if k - (7 - G) >= 1:
+            t.wait_ge(T.sem.act, cp_done[k - (7 - G)])
+        y_done[k] = done(t.matmul_mx(bank(out_bank(k), n), T.w2q[:], T.w2s[:],
+                                     T["hq%d" % c][:, :n], T["hs%d" % c][:, :n], True, True), "pe")
+        if k:
+            s.wait_ge(T.sem.pe, y_done[k])
+            cp_done[k] = done(s.activation(T["res%d" % c][:, :n], bank(out_bank(k), n), ActivationFunctionType.Copy), "act")
+            g.wait_ge(T.sem.act, cp_done[k])
+            home = T.cores[c]
+            hm = topo.mask(core, home)
+            hr, hp = topo.addr(home)[0], topo.addr(home)[1]
+            g.remote_dma(T["land%d" % r][:, :n], T["res%d" % c][:, :n], T.sem["y%d" % r], T.sem.sent, hp, hr, hm)
+            cnt["sent"] += engines(hm)
+
+    for k in range(NR):
+        first_product(k)
+        make_h(k)
+        if k:
+            second_product(k - 1)
+    second_product(NR - 1)
+
+    acc = bank(out_bank(0), W)
+    v.wait_ge(T.sem.pe, y_done[0])
+    for k in range(1, NR):
+        d = to[k]
+        v.wait_ge(T.sem["y%d" % d], engines(topo.mask(T.cores[d], core)))
+        if k > 1:
+            v.wait_ge(T.sem.dve, cnt["dve"])
+        o = T["acc%d" % (k % 2)][:, :W]
+        done(v.tensor_tensor(o, T["land%d" % d][:, :W], acc, AluOpType.add), "dve")
+        acc = o
+    g.sync.wait_ge(T.sem.dve, cnt["dve"])
+    g.sync.dma_start(T.y[:, :W], acc).then_inc(T.sem.stored, 16)
+    g.sync.wait_ge(T.sem.stored, 16)
+    g.wait_ge(T.sem.sent, cnt["sent"])

@@ -3,10 +3,16 @@ from concourse.bass import DstId, RemoteDMATransfer
 from concourse.mybir import dt, AluOpType, ActivationFunctionType
 
 NR = 5
+NCORES = 96
 WMAX = 256
 G = 4
 C = float(np.float32(0.041))
 BANK = 512
+MINCOL = 128
+W1PARTS = 2
+
+DIRECT = [1, 2, 3]
+RELAYED = 4
 
 SCRATCH = {
     "xt": ("sbuf", [128, 4 * WMAX], "bfloat16"),
@@ -29,8 +35,10 @@ for _k in range(NR):
     SCRATCH["res%d" % _k] = ("sbuf", [128, WMAX], "float32")
     SCRATCH["land%d" % _k] = ("sbuf", [128, WMAX], "float32")
 
-SEMAPHORES = ["ldx", "ldw1", "ldw2", "pe", "act", "dve", "sent", "stored"]
-SEMAPHORES += ["x%d" % k for k in range(NR)] + ["y%d" % k for k in range(NR)]
+SEMAPHORES = ["ldx", "ldw2", "pe", "act", "dve", "sent", "hp", "hc", "st0", "st1"]
+SEMAPHORES += ["ldw1%d" % k for k in range(W1PARTS)]
+SEMAPHORES += ["p%d" % k for k in range(NR)] + ["c%d" % k for k in range(NR)]
+SEMAPHORES += ["y%d%d" % (k, j) for k in range(NR) for j in range(2)]
 
 
 def engines(mask):
@@ -38,14 +46,51 @@ def engines(mask):
 
 
 def rank_program(g, core, T, topo):
-    r = T.rank_of(core)
-    if r is None:
-        return
     WID = T.tables["WID"]
+    r = T.rank_of(core)
+    sent = [0]
+
+    def helper(rr):
+        own = T.cores[rr]
+        return [q for q in range(NCORES) if topo.chip(q) == topo.chip(own) and topo.die(q) != topo.die(own)][0]
+
+    def hop_mask(rr):
+        src = T.cores[rr]
+        m = topo.mask(src, helper(rr))
+        for d in T.cores:
+            if d != src:
+                m &= ~topo.mask(src, d)
+        return m
+
+    def put(out, in_, sem, dst, mask):
+        a = topo.addr(dst)
+        g.remote_dma(out, in_, T.sem[sem], T.sem.sent, a[1], a[0], mask)
+        sent[0] += engines(mask)
+
+    def tokens(rr, dst, mask, psem, csem):
+        p = T["xs%d" % rr][:, :WID[rr]]
+        q = T["xq%d" % rr][:, :WID[rr]].bitcast(dt.uint8)
+        put(p, p, psem, dst, mask)
+        put(q, q, csem, dst, mask)
+
+    if r is None:
+        for rr in range(NR):
+            if core == helper(rr):
+                dst = T.cores[(rr + RELAYED) % NR]
+                m, n = topo.mask(core, dst), engines(hop_mask(rr))
+                p = T["xs%d" % rr][:, :WID[rr]]
+                q = T["xq%d" % rr][:, :WID[rr]].bitcast(dt.uint8)
+                g.wait_ge(T.sem.hp, n)
+                put(p, p, "p%d" % rr, dst, m)
+                g.wait_ge(T.sem.hc, n)
+                put(q, q, "c%d" % rr, dst, m)
+                g.wait_ge(T.sem.sent, sent[0])
+        return
+
     W = WID[r]
     to = [(r + k) % NR for k in range(NR)]
     frm = [(r - k) % NR for k in range(NR)]
-    cnt = {"pe": 0, "act": 0, "dve": 0, "sent": 0}
+    cnt = {"pe": 0, "act": 0, "dve": 0}
     v, s, t = g.vector, g.scalar, g.tensor
 
     def done(ins, sem):
@@ -56,117 +101,120 @@ def rank_program(g, core, T, topo):
     def bank(i, n):
         return T.ps[:, BANK * i:BANK * i + n]
 
+    def parts(n):
+        if n >= 2 * MINCOL:
+            return [(0, n // 2), (n // 2, n - n // 2)]
+        return [(0, n)]
+
     g.sync.dma_start(T.xt[:, :4 * W], T.x[:, :4 * W]).then_inc(T.sem.ldx, 16)
-    g.sync.dma_start(T.w1t[:], T.w1[:]).then_inc(T.sem.ldw1, 16)
+    per = G // W1PARTS
+    for i in range(W1PARTS):
+        a, b = 512 * per * i, 512 * per * (i + 1)
+        g.sync.dma_start(T.w1t[:, a:b], T.w1[:, a:b]).then_inc(T.sem["ldw1%d" % i], 16)
     g.sync.dma_start(T.w2t[:], T.w2[:]).then_inc(T.sem.ldw2, 16)
 
-    xq, xs = T["xq%d" % r], T["xs%d" % r]
     v.wait_ge(T.sem.ldx, 16)
-    x_ready = done(v.quantize_mx(xq[:, :W], xs[:, :W], T.xt[:, :4 * W]), "dve")
-    v.wait_ge(T.sem.ldw1, 16)
-    w1_ready = [done(v.quantize_mx(T.w1q[:, 128 * b:128 * b + 128], T.w1s[:, 128 * b:128 * b + 128],
-                                   T.w1t[:, 512 * b:512 * b + 512]), "dve") for b in range(G)]
-    v.wait_ge(T.sem.ldw2, 16)
-    done(v.quantize_mx(T.w2q[:], T.w2s[:], T.w2t[:]), "dve")
+    x_ready = done(v.quantize_mx(T["xq%d" % r][:, :W], T["xs%d" % r][:, :W], T.xt[:, :4 * W]), "dve")
+    w1_ready = []
+    for b in range(G):
+        if b % per == 0:
+            v.wait_ge(T.sem["ldw1%d" % (b // per)], 16)
+        w1_ready.append(done(v.quantize_mx(T.w1q[:, 128 * b:128 * b + 128], T.w1s[:, 128 * b:128 * b + 128],
+                                           T.w1t[:, 512 * b:512 * b + 512]), "dve"))
 
     g.wait_ge(T.sem.dve, x_ready)
-    dst = [T.cores[d] for d in to]
-    rid = [topo.addr(c)[0] for c in dst]
-    pid = [topo.addr(c)[1] for c in dst]
-    msk = [0] + [topo.mask(core, dst[k]) for k in range(1, NR)]
-    every = msk[1]
-    for k in range(2, NR):
-        every &= msk[k]
-    g.remote_dma_fused([RemoteDMATransfer(
-        dst_ids=[DstId(rid=rid[k], pnc=pid[k]) for k in range(1, NR)], dma_engine_mask=every,
-        remote_sem=T.sem["x%d" % r], srcs=[xs[:, :W]], dsts=[xs[:, :W] for k in range(1, NR)])], local_sem=T.sem.sent)
-    cnt["sent"] += engines(every)
+    for k in DIRECT:
+        dst = T.cores[to[k]]
+        tokens(r, dst, topo.mask(core, dst), "p%d" % r, "c%d" % r)
+        if k == DIRECT[0]:
+            tokens(r, helper(r), hop_mask(r), "hp", "hc")
+
+    units = [(0, r, 0, W, 0)]
     for k in range(1, NR):
-        g.remote_dma(xq[:, :W].bitcast(dt.uint8), xq[:, :W].bitcast(dt.uint8), T.sem["x%d" % r], T.sem.sent,
-                     pid[k], rid[k], msk[k])
-        cnt["sent"] += engines(msk[k])
+        units += [(k, frm[k], a, n, j) for j, (a, n) in enumerate(parts(WID[frm[k]]))]
+    NU = len(units)
+    z_done = [[0] * G for u in units]
+    act_done = [[None] * G for u in units]
+    q_done, y_done, cp_done = [0] * NU, [0] * NU, [0] * NU
+    w2_ready = [0]
 
-    z_done = [[0] * G for k in range(NR)]
-    act_done = [[None] * G for k in range(NR)]
-    q_done = [0] * NR
-    y_done = [0] * NR
-    cp_done = [0] * NR
-
-    def first_product(k):
-        c = frm[k]
-        n = WID[c]
-        if k:
-            sender = T.cores[c]
-            em = topo.mask(sender, core)
-            for o in T.cores:
-                if o != sender:
-                    em &= topo.mask(sender, o)
-            t.wait_ge(T.sem["x%d" % c], engines(em) + engines(topo.mask(sender, core)))
+    def first_product(u):
+        k, c, a, n, j = units[u]
+        if k and j == 0:
+            src = helper(c) if k == RELAYED else T.cores[c]
+            t.wait_ge(T.sem["p%d" % c], engines(topo.mask(src, core)))
+            t.wait_ge(T.sem["c%d" % c], engines(topo.mask(src, core)))
         for b in range(G):
-            if k == 0:
+            if u == 0:
                 t.wait_ge(T.sem.dve, w1_ready[b])
             else:
-                sem, val = act_done[k - 1][b]
+                sem, val = act_done[u - 1][b]
                 t.wait_ge(T.sem[sem], val)
-            z_done[k][b] = done(t.matmul_mx(bank(b, n), T.w1q[:, 128 * b:128 * b + 128], T.w1s[:, 128 * b:128 * b + 128],
-                                            T["xq%d" % c][:, :n], T["xs%d" % c][:, :n], True, True), "pe")
+            z_done[u][b] = done(t.matmul_mx(bank(b, n), T.w1q[:, 128 * b:128 * b + 128],
+                                            T.w1s[:, 128 * b:128 * b + 128], T["xq%d" % c][:, a:a + n],
+                                            T["xs%d" % c][:, a:a + n], True, True), "pe")
 
-    def make_h(k):
-        c = frm[k]
-        n = WID[c]
+    def make_h(u):
+        k, c, a, n, j = units[u]
         h = T["h%d" % c]
         for b in range(G):
+            o = h[:, 4 * a + b:4 * (a + n):4]
             if b % 2 == 0:
-                s.wait_ge(T.sem.pe, z_done[k][b])
-                act_done[k][b] = ("act", done(s.activation(h[:, b:4 * n:4], bank(b, n), ActivationFunctionType.Relu,
-                                                           scale=C), "act"))
+                s.wait_ge(T.sem.pe, z_done[u][b])
+                act_done[u][b] = ("act", done(s.activation(o, bank(b, n), ActivationFunctionType.Relu, scale=C), "act"))
             else:
-                v.wait_ge(T.sem.pe, z_done[k][b])
-                act_done[k][b] = ("dve", done(v.tensor_scalar(h[:, b:4 * n:4], bank(b, n), 0.0, C,
-                                                              AluOpType.max, AluOpType.mult), "dve"))
-        v.wait_ge(T.sem.act, cnt["act"])
-        v.wait_ge(T.sem.dve, cnt["dve"])
-        q_done[k] = done(v.quantize_mx(T["hq%d" % c][:, :n], T["hs%d" % c][:, :n], h[:, :4 * n]), "dve")
+                v.wait_ge(T.sem.pe, z_done[u][b])
+                act_done[u][b] = ("dve", done(v.tensor_scalar(o, bank(b, n), 0.0, C, AluOpType.max, AluOpType.mult), "dve"))
+        v.wait_ge(T.sem.act, act_done[u][2][1])
+        v.wait_ge(T.sem.dve, act_done[u][3][1])
+        q_done[u] = done(v.quantize_mx(T["hq%d" % c][:, a:a + n], T["hs%d" % c][:, a:a + n],
+                                       h[:, 4 * a:4 * (a + n)]), "dve")
 
-    def out_bank(k):
-        return G if k == 0 else G + 1 + (k - 1) % (7 - G)
+    def out_bank(u):
+        return G if u == 0 else G + 1 + (u - 1) % (7 - G)
 
-    def second_product(k):
-        c = frm[k]
-        n = WID[c]
-        t.wait_ge(T.sem.dve, q_done[k])
-        if k - (7 - G) >= 1:
-            t.wait_ge(T.sem.act, cp_done[k - (7 - G)])
-        y_done[k] = done(t.matmul_mx(bank(out_bank(k), n), T.w2q[:], T.w2s[:],
-                                     T["hq%d" % c][:, :n], T["hs%d" % c][:, :n], True, True), "pe")
+    def second_product(u):
+        k, c, a, n, j = units[u]
+        t.wait_ge(T.sem.dve, q_done[u])
+        if u == 0:
+            t.wait_ge(T.sem.dve, w2_ready[0])
+        if u - (7 - G) >= 1:
+            t.wait_ge(T.sem.act, cp_done[u - (7 - G)])
+        y_done[u] = done(t.matmul_mx(bank(out_bank(u), n), T.w2q[:], T.w2s[:], T["hq%d" % c][:, a:a + n],
+                                     T["hs%d" % c][:, a:a + n], True, True), "pe")
         if k:
-            s.wait_ge(T.sem.pe, y_done[k])
-            cp_done[k] = done(s.activation(T["res%d" % c][:, :n], bank(out_bank(k), n), ActivationFunctionType.Copy), "act")
-            g.wait_ge(T.sem.act, cp_done[k])
-            home = T.cores[c]
-            hm = topo.mask(core, home)
-            hr, hp = topo.addr(home)[0], topo.addr(home)[1]
-            g.remote_dma(T["land%d" % r][:, :n], T["res%d" % c][:, :n], T.sem["y%d" % r], T.sem.sent, hp, hr, hm)
-            cnt["sent"] += engines(hm)
+            s.wait_ge(T.sem.pe, y_done[u])
+            cp_done[u] = done(s.activation(T["res%d" % c][:, a:a + n], bank(out_bank(u), n),
+                                           ActivationFunctionType.Copy), "act")
+            g.wait_ge(T.sem.act, cp_done[u])
+            put(T["land%d" % r][:, a:a + n], T["res%d" % c][:, a:a + n], "y%d%d" % (r, j), T.cores[c],
+                topo.mask(core, T.cores[c]))
 
-    for k in range(NR):
-        first_product(k)
-        make_h(k)
-        if k:
-            second_product(k - 1)
-    second_product(NR - 1)
+    for u in range(NU):
+        first_product(u)
+        make_h(u)
+        if u == 0:
+            v.wait_ge(T.sem.ldw2, 16)
+            w2_ready[0] = done(v.quantize_mx(T.w2q[:], T.w2s[:], T.w2t[:]), "dve")
+        else:
+            second_product(u - 1)
+    second_product(NU - 1)
 
-    acc = bank(out_bank(0), W)
     v.wait_ge(T.sem.pe, y_done[0])
+    acc = [T.ps[:, BANK * out_bank(0) + a:BANK * out_bank(0) + a + n] for a, n in parts(W)]
+    last = [0 for a in acc]
     for k in range(1, NR):
         d = to[k]
-        v.wait_ge(T.sem["y%d" % d], engines(topo.mask(T.cores[d], core)))
-        if k > 1:
-            v.wait_ge(T.sem.dve, cnt["dve"])
-        o = T["acc%d" % (k % 2)][:, :W]
-        done(v.tensor_tensor(o, T["land%d" % d][:, :W], acc, AluOpType.add), "dve")
-        acc = o
-    g.sync.wait_ge(T.sem.dve, cnt["dve"])
-    g.sync.dma_start(T.y[:, :W], acc).then_inc(T.sem.stored, 16)
-    g.sync.wait_ge(T.sem.stored, 16)
-    g.wait_ge(T.sem.sent, cnt["sent"])
+        for j, (a, n) in enumerate(parts(W)):
+            v.wait_ge(T.sem["y%d%d" % (d, j)], engines(topo.mask(T.cores[d], core)))
+            if k > 1:
+                v.wait_ge(T.sem.dve, last[j])
+            o = T["acc%d" % (k % 2)][:, a:a + n]
+            last[j] = done(v.tensor_tensor(o, T["land%d" % d][:, a:a + n], acc[j], AluOpType.add), "dve")
+            acc[j] = o
+    for j, (a, n) in enumerate(parts(W)):
+        g.sync.wait_ge(T.sem.dve, last[j])
+        g.sync.dma_start(T.y[:, a:a + n], acc[j]).then_inc(T.sem["st%d" % j], 16)
+    for j in range(len(acc)):
+        g.sync.wait_ge(T.sem["st%d" % j], 16)
+    g.wait_ge(T.sem.sent, sent[0])

import numpy as np
from concourse.bass import DstId, RemoteDMATransfer
from concourse.mybir import dt, AluOpType, ActivationFunctionType

NR = 5
NCORES = 96
WMAX = 256
G = 4
C = float(np.float32(0.041))
BANK = 512
MINCOL = 128
W1PARTS = 2

DIRECT = [1, 2, 3]
RELAYED = 4

SCRATCH = {
    "xt": ("sbuf", [128, 4 * WMAX], "bfloat16"),
    "w1t": ("sbuf", [128, G * 512], "bfloat16"),
    "w2t": ("sbuf", [128, 512], "bfloat16"),
    "w1q": ("sbuf", [128, G * 128], "float8_e4m3fn_x4"),
    "w1s": ("sbuf", [128, G * 128], "uint8"),
    "w2q": ("sbuf", [128, 128], "float8_e4m3fn_x4"),
    "w2s": ("sbuf", [128, 128], "uint8"),
    "acc0": ("sbuf", [128, WMAX], "float32"),
    "acc1": ("sbuf", [128, WMAX], "float32"),
    "ps": ("psum", [128, 8 * BANK], "float32"),
}
for _k in range(NR):
    SCRATCH["xq%d" % _k] = ("sbuf", [128, WMAX], "float8_e4m3fn_x4")
    SCRATCH["xs%d" % _k] = ("sbuf", [128, WMAX], "uint8")
    SCRATCH["h%d" % _k] = ("sbuf", [128, 4 * WMAX], "bfloat16")
    SCRATCH["hq%d" % _k] = ("sbuf", [128, WMAX], "float8_e4m3fn_x4")
    SCRATCH["hs%d" % _k] = ("sbuf", [128, WMAX], "uint8")
    SCRATCH["res%d" % _k] = ("sbuf", [128, WMAX], "float32")
    SCRATCH["land%d" % _k] = ("sbuf", [128, WMAX], "float32")

SEMAPHORES = ["ldx", "ldw2", "pe", "act", "dve", "sent", "hp", "hc", "st0", "st1"]
SEMAPHORES += ["ldw1%d" % k for k in range(W1PARTS)]
SEMAPHORES += ["p%d" % k for k in range(NR)] + ["c%d" % k for k in range(NR)]
SEMAPHORES += ["y%d%d" % (k, j) for k in range(NR) for j in range(2)]


def engines(mask):
    return bin(mask).count("1")


def rank_program(g, core, T, topo):
    WID = T.tables["WID"]
    r = T.rank_of(core)
    sent = [0]

    def helper(rr):
        own = T.cores[rr]
        return [q for q in range(NCORES) if topo.chip(q) == topo.chip(own) and topo.die(q) != topo.die(own)][0]

    def hop_mask(rr):
        src = T.cores[rr]
        m = topo.mask(src, helper(rr))
        for d in T.cores:
            if d != src:
                m &= ~topo.mask(src, d)
        return m

    def put(out, in_, sem, dst, mask):
        a = topo.addr(dst)
        g.remote_dma(out, in_, T.sem[sem], T.sem.sent, a[1], a[0], mask)
        sent[0] += engines(mask)

    def tokens(rr, dst, mask, psem, csem):
        p = T["xs%d" % rr][:, :WID[rr]]
        q = T["xq%d" % rr][:, :WID[rr]].bitcast(dt.uint8)
        put(p, p, psem, dst, mask)
        put(q, q, csem, dst, mask)

    if r is None:
        for rr in range(NR):
            if core == helper(rr):
                dst = T.cores[(rr + RELAYED) % NR]
                m, n = topo.mask(core, dst), engines(hop_mask(rr))
                p = T["xs%d" % rr][:, :WID[rr]]
                q = T["xq%d" % rr][:, :WID[rr]].bitcast(dt.uint8)
                g.wait_ge(T.sem.hp, n)
                put(p, p, "p%d" % rr, dst, m)
                g.wait_ge(T.sem.hc, n)
                put(q, q, "c%d" % rr, dst, m)
                g.wait_ge(T.sem.sent, sent[0])
        return

    W = WID[r]
    to = [(r + k) % NR for k in range(NR)]
    frm = [(r - k) % NR for k in range(NR)]
    cnt = {"pe": 0, "act": 0, "dve": 0}
    v, s, t = g.vector, g.scalar, g.tensor

    def done(ins, sem):
        ins.then_inc(T.sem[sem], 1)
        cnt[sem] += 1
        return cnt[sem]

    def bank(i, n):
        return T.ps[:, BANK * i:BANK * i + n]

    def parts(n):
        if n >= 2 * MINCOL:
            return [(0, n // 2), (n // 2, n - n // 2)]
        return [(0, n)]

    g.sync.dma_start(T.xt[:, :4 * W], T.x[:, :4 * W]).then_inc(T.sem.ldx, 16)
    per = G // W1PARTS
    for i in range(W1PARTS):
        a, b = 512 * per * i, 512 * per * (i + 1)
        g.sync.dma_start(T.w1t[:, a:b], T.w1[:, a:b]).then_inc(T.sem["ldw1%d" % i], 16)
    g.sync.dma_start(T.w2t[:], T.w2[:]).then_inc(T.sem.ldw2, 16)

    v.wait_ge(T.sem.ldx, 16)
    x_ready = done(v.quantize_mx(T["xq%d" % r][:, :W], T["xs%d" % r][:, :W], T.xt[:, :4 * W]), "dve")
    w1_ready = []
    for b in range(G):
        if b % per == 0:
            v.wait_ge(T.sem["ldw1%d" % (b // per)], 16)
        w1_ready.append(done(v.quantize_mx(T.w1q[:, 128 * b:128 * b + 128], T.w1s[:, 128 * b:128 * b + 128],
                                           T.w1t[:, 512 * b:512 * b + 512]), "dve"))

    g.wait_ge(T.sem.dve, x_ready)
    for k in DIRECT:
        dst = T.cores[to[k]]
        tokens(r, dst, topo.mask(core, dst), "p%d" % r, "c%d" % r)
        if k == DIRECT[0]:
            tokens(r, helper(r), hop_mask(r), "hp", "hc")

    units = [(0, r, 0, W, 0)]
    for k in range(1, NR):
        units += [(k, frm[k], a, n, j) for j, (a, n) in enumerate(parts(WID[frm[k]]))]
    NU = len(units)
    z_done = [[0] * G for u in units]
    act_done = [[None] * G for u in units]
    q_done, y_done, cp_done = [0] * NU, [0] * NU, [0] * NU
    w2_ready = [0]

    def first_product(u):
        k, c, a, n, j = units[u]
        if k and j == 0:
            src = helper(c) if k == RELAYED else T.cores[c]
            t.wait_ge(T.sem["p%d" % c], engines(topo.mask(src, core)))
            t.wait_ge(T.sem["c%d" % c], engines(topo.mask(src, core)))
        for b in range(G):
            if u == 0:
                t.wait_ge(T.sem.dve, w1_ready[b])
            else:
                sem, val = act_done[u - 1][b]
                t.wait_ge(T.sem[sem], val)
            z_done[u][b] = done(t.matmul_mx(bank(b, n), T.w1q[:, 128 * b:128 * b + 128],
                                            T.w1s[:, 128 * b:128 * b + 128], T["xq%d" % c][:, a:a + n],
                                            T["xs%d" % c][:, a:a + n], True, True), "pe")

    def make_h(u):
        k, c, a, n, j = units[u]
        h = T["h%d" % c]
        for b in range(G):
            o = h[:, 4 * a + b:4 * (a + n):4]
            if b % 2 == 0:
                s.wait_ge(T.sem.pe, z_done[u][b])
                act_done[u][b] = ("act", done(s.activation(o, bank(b, n), ActivationFunctionType.Relu, scale=C), "act"))
            else:
                v.wait_ge(T.sem.pe, z_done[u][b])
                act_done[u][b] = ("dve", done(v.tensor_scalar(o, bank(b, n), 0.0, C, AluOpType.max, AluOpType.mult), "dve"))
        v.wait_ge(T.sem.act, act_done[u][2][1])
        v.wait_ge(T.sem.dve, act_done[u][3][1])
        q_done[u] = done(v.quantize_mx(T["hq%d" % c][:, a:a + n], T["hs%d" % c][:, a:a + n],
                                       h[:, 4 * a:4 * (a + n)]), "dve")

    def out_bank(u):
        return G if u == 0 else G + 1 + (u - 1) % (7 - G)

    def second_product(u):
        k, c, a, n, j = units[u]
        t.wait_ge(T.sem.dve, q_done[u])
        if u == 0:
            t.wait_ge(T.sem.dve, w2_ready[0])
        if u - (7 - G) >= 1:
            t.wait_ge(T.sem.act, cp_done[u - (7 - G)])
        y_done[u] = done(t.matmul_mx(bank(out_bank(u), n), T.w2q[:], T.w2s[:], T["hq%d" % c][:, a:a + n],
                                     T["hs%d" % c][:, a:a + n], True, True), "pe")
        if k:
            s.wait_ge(T.sem.pe, y_done[u])
            cp_done[u] = done(s.activation(T["res%d" % c][:, a:a + n], bank(out_bank(u), n),
                                           ActivationFunctionType.Copy), "act")
            g.wait_ge(T.sem.act, cp_done[u])
            put(T["land%d" % r][:, a:a + n], T["res%d" % c][:, a:a + n], "y%d%d" % (r, j), T.cores[c],
                topo.mask(core, T.cores[c]))

    for u in range(NU):
        first_product(u)
        make_h(u)
        if u == 0:
            v.wait_ge(T.sem.ldw2, 16)
            w2_ready[0] = done(v.quantize_mx(T.w2q[:], T.w2s[:], T.w2t[:]), "dve")
        else:
            second_product(u - 1)
    second_product(NU - 1)

    v.wait_ge(T.sem.pe, y_done[0])
    acc = [T.ps[:, BANK * out_bank(0) + a:BANK * out_bank(0) + a + n] for a, n in parts(W)]
    last = [0 for a in acc]
    for k in range(1, NR):
        d = to[k]
        for j, (a, n) in enumerate(parts(W)):
            v.wait_ge(T.sem["y%d%d" % (d, j)], engines(topo.mask(T.cores[d], core)))
            if k > 1:
                v.wait_ge(T.sem.dve, last[j])
            o = T["acc%d" % (k % 2)][:, a:a + n]
            last[j] = done(v.tensor_tensor(o, T["land%d" % d][:, a:a + n], acc[j], AluOpType.add), "dve")
            acc[j] = o
    for j, (a, n) in enumerate(parts(W)):
        g.sync.wait_ge(T.sem.dve, last[j])
        g.sync.dma_start(T.y[:, a:a + n], acc[j]).then_inc(T.sem["st%d" % j], 16)
    for j in range(len(acc)):
        g.sync.wait_ge(T.sem["st%d" % j], 16)
    g.wait_ge(T.sem.sent, sent[0])
